import numpy as np, ml_dtypes
CORES = [37,45,53,61,69,109,117,125]
N = 8
TK = 256
WID = [32,256,32,224,32,128,192,32]
def setup_inputs(rng):
    rt = (0.75 * rng.standard_normal((128, 1), dtype=np.float32) + rng.standard_normal((128, N), dtype=np.float32) / 2).astype(ml_dtypes.bfloat16)
    return {"x": rng.standard_normal((N, 128, TK), dtype=np.float32).astype(ml_dtypes.bfloat16), "rt": np.broadcast_to(rt, (N, 128, N)).copy(), "w": rng.standard_normal((N, 128, 128), dtype=np.float32).astype(ml_dtypes.bfloat16)}
def setup_inputs_big(rng):
    d = setup_inputs(rng)
    for k in ("x", "w"): d[k] = (d[k].astype(np.float32) * 1024.0).astype(d[k].dtype)
    return d
def setup_inputs_small(rng):
    d = setup_inputs(rng)
    for k in ("x", "w"): d[k] = (d[k].astype(np.float32) * (1 / 1024.0)).astype(d[k].dtype)
    return d
def whole(x, rt, w):
    X, RT, W = x.astype(np.float64), rt.astype(np.float64), w.astype(np.float64)
    y = np.zeros((N, 128, TK))
    for r in range(N):
        sc = RT[r].T @ X[r]
        g = np.exp(sc - sc.max(axis=0)); g = g / g.sum(axis=0)
        y[r] = sum(g[j] * (W[j].T @ X[r]) for j in range(N))
    return {"y": y.astype(ml_dtypes.bfloat16)}
def reference(x, rt, w):
    o = whole(x, rt, w)["y"].copy()
    for r in range(N):
        o[r][:, WID[r]:] = np.nan
    return {"y": o}

@@ -1,0 +1,220 @@
+from concourse.bass import DstId, RemoteDMATransfer
+from concourse.mybir import dt, AluOpType, AxisListType, ActivationFunctionType
+
+NH = 2
+NE = 8
+NG = 4
+
+SCRATCH = {
+    "wall": ("sbuf", [128, 1024], "bfloat16"),
+    "hw": ("sbuf", [128, 128], "bfloat16"),
+    "xs": ("sbuf", [128, 256], "bfloat16"),
+    "rts": ("sbuf", [128, 8], "bfloat16"),
+    "ones": ("sbuf", [128, 128], "bfloat16"),
+    "ident": ("sbuf", [128, 128], "bfloat16"),
+    "nm": ("sbuf", [128, 2], "float32"),
+    "ex": ("sbuf", [128, 16], "float32"),
+    "ssum": ("sbuf", [128, 2], "float32"),
+    "rs": ("sbuf", [128, 2], "float32"),
+    "xtg": ("sbuf", [128, 2048], "bfloat16"),
+    "xg": ("sbuf", [128, 2048], "bfloat16"),
+    "ysb": ("sbuf", [128, 256], "bfloat16"),
+    "pa": ("psum", [128, 512], "float32"),
+    "pb": ("psum", [128, 512], "float32"),
+    "xtp": ("psum", [128, 1024], "bfloat16"),
+    "xgp0": ("psum", [128, 1024], "bfloat16"),
+    "xgp1": ("psum", [128, 1024], "bfloat16"),
+    "xgp2": ("psum", [128, 1024], "bfloat16"),
+    "xgp3": ("psum", [128, 1024], "bfloat16"),
+}
+SEMAPHORES = (["ldw", "ldx", "ldr", "fill", "idn", "ssc", "sxt", "snm", "sex", "srs", "sy0", "sy1", "sev", "st",
+               "sent", "ha", "hs"]
+              + ["a%d" % j for j in range(8)]
+              + ["sl%d" % k for k in range(NG)] + ["tr%d" % k for k in range(NG)] + ["xr%d" % k for k in range(NG)])
+
+
+def _engines(mask, n):
+    out, bit = 0, 1
+    while n > 0 and bit <= mask:
+        if mask & bit:
+            out |= bit
+            n -= 1
+        bit <<= 1
+    return out
+
+
+def _plan(T, topo):
+    cores = list(T.cores)
+    n = len(cores)
+    plan = []
+    for r, c in enumerate(cores):
+        plane = [j for j in range(n) if j == r or topo.may_write(c, cores[j])]
+        cross = [j for j in range(n) if j not in plane]
+        k = plane.index(r)
+        direct = [plane[(k + i) % len(plane)] for i in range(1, len(plane))]
+        if cross:
+            s = k % len(cross)
+            cross = cross[s:] + cross[:s]
+        cand = [h for h in range(topo.CHIPS * topo.CORES_PER_CHIP)
+                if topo.chip(h) == topo.chip(c) and h not in cores
+                and all(topo.may_write(h, cores[j]) for j in cross)]
+        cand.sort(key=lambda h: (topo.die(h) != topo.die(c), h))
+        helpers = cand[:NH] if cross else []
+        per = (len(cross) + len(helpers) - 1) // len(helpers) if helpers else 0
+        shares = [cross[i * per:(i + 1) * per] for i in range(len(helpers))]
+        plan.append({"direct": direct, "helpers": helpers, "shares": shares})
+    return plan
+
+
+def _send(g, T, topo, core, src, dst_cores, dst_ap, sem, local_sem):
+    mask = 0
+    for i, d in enumerate(dst_cores):
+        m = topo.mask(core, d)
+        mask = m if i == 0 else (mask & m)
+    ids = []
+    for d in dst_cores:
+        rid, pid, _s = topo.addr(d)
+        ids.append(DstId(rid=rid, pnc=pid))
+    g.remote_dma_fused([RemoteDMATransfer(dst_ids=ids, dma_engine_mask=_engines(mask, NE), remote_sem=sem,
+                                          srcs=[src], dsts=[dst_ap for _d in dst_cores], alu_op=0)],
+                       local_sem=local_sem)
+
+
+def rank_program(g, core, T, topo):
+    plan = _plan(T, topo)
+    cores = list(T.cores)
+    S = T.sem
+    rank = T.rank_of(core)
+
+    if rank is None:
+        for r, p in enumerate(plan):
+            if core in p["helpers"]:
+                share = p["shares"][p["helpers"].index(core)]
+                if not share:
+                    continue
+                g.wait_ge(S.ha, NE)
+                _send(g, T, topo, core, T.hw[:], [cores[j] for j in share],
+                      T.wall[:, r * 128:(r + 1) * 128], S["a%d" % r], S.hs)
+                g.wait_ge(S.hs, NE)
+        return
+
+    me = plan[rank]
+    n = len(cores)
+    Tn = int(T.tables["WID"][rank])
+    blocks = [(s, min(128, Tn - s)) for s in range(0, Tn, 128)]
+    nb = len(blocks)
+    myw = T.wall[:, rank * 128:(rank + 1) * 128]
+    V, SC, TE, SY = g.vector, g.scalar, g.tensor, g.sync
+
+    def when(j):
+        if j == rank:
+            return (0, 0)
+        if rank in plan[j]["direct"]:
+            return (1, plan[j]["direct"].index(rank))
+        for sh in plan[j]["shares"]:
+            if rank in sh:
+                return (2, sh.index(rank))
+        return (3, 0)
+    order = sorted(range(n), key=lambda j: (when(j), j))
+    per_g = n // NG
+
+    SY.dma_start(myw, T.w[:, :]).then_inc(S.ldw, 16)
+    SC.dma_start(T.xs[:, 0:Tn], T.x[:, 0:Tn]).then_inc(S.ldx, 16)
+    SY.dma_start(T.rts[:, :], T.rt[:, :]).then_inc(S.ldr, 16)
+
+    V.memset(T.ones[:], 1.0).then_inc(S.fill, 1)
+    V.memset(T.ssum[:], 1.0).then_inc(S.fill, 1)
+    g.wait_ge(S.fill, 2)
+    g.affine_select(T.ident[:], T.ones[:], [[-1, 128]], AluOpType.is_equal, 0.0, 0, 1).then_inc(S.idn, 1)
+
+    g.wait_ge(S.ldw, 16)
+    sent = 0
+    if me["helpers"]:
+        _send(g, T, topo, core, myw, me["helpers"], T.hw[:], S.ha, S.sent)
+        sent += NE
+    if me["direct"]:
+        _send(g, T, topo, core, myw, [cores[j] for j in me["direct"]], myw, S["a%d" % rank], S.sent)
+        sent += NE
+
+    TE.wait_ge(S.ldx, 16)
+    TE.wait_ge(S.ldr, 16)
+    for b, (s, tb) in enumerate(blocks):
+        TE.matmul(T.pa[0:tb, 256 + b * 8:256 + (b + 1) * 8], T.xs[:, s:s + tb], T.rts[:, :], True, True
+                  ).then_inc(S.ssc, 1)
+    TE.wait_ge(S.idn, 1)
+    for b, (s, tb) in enumerate(blocks):
+        TE.transpose(T.xtp[0:tb, b * 128:(b + 1) * 128], T.xs[:, s:s + tb], T.ident[:, :]).then_inc(S.sxt, 1)
+
+    V.wait_ge(S.ssc, nb)
+    for b, (s, tb) in enumerate(blocks):
+        V.tensor_reduce(T.nm[0:tb, b:b + 1], T.pa[0:tb, 256 + b * 8:256 + (b + 1) * 8], AxisListType.X,
+                        AluOpType.max, negate=True).then_inc(S.snm, 1)
+    SC.wait_ge(S.fill, 2)
+    SC.wait_ge(S.ssc, nb)
+    SC.wait_ge(S.snm, nb)
+    for b, (s, tb) in enumerate(blocks):
+        SC.activation(T.ex[0:tb, b * 8:(b + 1) * 8], T.pa[0:tb, 256 + b * 8:256 + (b + 1) * 8],
+                      ActivationFunctionType.Exp, bias=T.nm[0:tb, b:b + 1], scale=1.0,
+                      accum_out=T.ssum[0:tb, b:b + 1]).then_inc(S.sex, 1)
+    V.wait_ge(S.fill, 2)
+    V.wait_ge(S.sex, nb)
+    V.reciprocal(T.rs[:, 0:nb], T.ssum[:, 0:nb]).then_inc(S.srs, 1)
+    V.wait_ge(S.srs, 1)
+    V.wait_ge(S.sxt, nb)
+
+    for k in range(NG):
+        for i in range(per_g):
+            j = order[k * per_g + i]
+            for b, (s, tb) in enumerate(blocks):
+                slot = (k * per_g + i) * nb + b
+                V.tensor_scalar(T.xtg[0:tb, slot * 128:(slot + 1) * 128], T.xtp[0:tb, b * 128:(b + 1) * 128],
+                                T.ex[0:tb, b * 8 + j:b * 8 + j + 1], T.rs[0:tb, b:b + 1],
+                                AluOpType.mult, AluOpType.mult).then_inc(S["sl%d" % k], 1)
+    for k in range(NG):
+        TE.wait_ge(S["sl%d" % k], per_g * nb)
+        for i in range(per_g):
+            for b, (s, tb) in enumerate(blocks):
+                slot = (k * per_g + i) * nb + b
+                TE.transpose(T["xgp%d" % k][:, i * Tn + s:i * Tn + s + tb],
+                             T.xtg[0:tb, slot * 128:(slot + 1) * 128], T.ident[0:tb, 0:tb]
+                             ).then_inc(S["tr%d" % k], 1)
+    for k in range(NG):
+        out = T.xg[:, k * per_g * Tn:(k + 1) * per_g * Tn]
+        src = T["xgp%d" % k][:, 0:per_g * Tn]
+        if k % 2 == 0:
+            SC.wait_ge(S["tr%d" % k], per_g * nb)
+            SC.activation(out, src, ActivationFunctionType.Copy).then_inc(S["xr%d" % k], 1)
+        else:
+            V.wait_ge(S["tr%d" % k], per_g * nb)
+            V.tensor_copy(out, src).then_inc(S["xr%d" % k], 1)
+
+    if Tn >= 128:
+        ta = ((Tn // 2 + 7) // 8) * 8
+        halves = [(0, ta, T.pa, S.sy0), (ta, Tn, T.pb, S.sy1)]
+    else:
+        halves = [(0, Tn, T.pa, S.sy0)]
+    for i, j in enumerate(order):
+        if i % per_g == 0:
+            TE.wait_ge(S["xr%d" % (i // per_g)], 1)
+        if j == rank:
+            TE.wait_ge(S.ldw, 16)
+        else:
+            TE.wait_ge(S["a%d" % j], NE)
+        for (lo, hi, ps, sem) in halves:
+            mm = TE.matmul(ps[:, 0:hi - lo], T.wall[:, j * 128:(j + 1) * 128], T.xg[:, i * Tn + lo:i * Tn + hi],
+                           i == 0, i == n - 1)
+            if i == n - 1:
+                mm.then_inc(sem, 1)
+
+    lo, hi, ps, sem = halves[0]
+    V.wait_ge(sem, 1)
+    V.tensor_copy(T.ysb[:, lo:hi], ps[:, 0:hi - lo]).then_inc(S.sev, 1)
+    if len(halves) > 1:
+        lo, hi, ps, sem = halves[1]
+        SC.wait_ge(sem, 1)
+        SC.activation(T.ysb[:, lo:hi], ps[:, 0:hi - lo], ActivationFunctionType.Copy).then_inc(S.sev, 1)
+    SY.wait_ge(S.sev, len(halves))
+    SY.dma_start(T.y[:, 0:Tn], T.ysb[:, 0:Tn]).then_inc(S.st, 16)
+    SY.wait_ge(S.st, 16)
+    if sent:
+        g.wait_ge(S.sent, sent)

@@ -6,8 +6,9 @@ NE = 8
 NG = 4
 
 SCRATCH = {
+    "wd": ("dram", [128, 128], "bfloat16"),
+    "hd": ("dram", [128, 128], "bfloat16"),
     "wall": ("sbuf", [128, 1024], "bfloat16"),
-    "hw": ("sbuf", [128, 128], "bfloat16"),
     "xs": ("sbuf", [128, 256], "bfloat16"),
     "rts": ("sbuf", [128, 8], "bfloat16"),
     "ones": ("sbuf", [128, 128], "bfloat16"),
@@ -15,6 +16,7 @@ SCRATCH = {
     "nm": ("sbuf", [128, 2], "float32"),
     "ex": ("sbuf", [128, 16], "float32"),
     "ssum": ("sbuf", [128, 2], "float32"),
+    "zz": ("sbuf", [128, 2], "float32"),
     "rs": ("sbuf", [128, 2], "float32"),
     "xtg": ("sbuf", [128, 2048], "bfloat16"),
     "xg": ("sbuf", [128, 2048], "bfloat16"),
@@ -27,8 +29,8 @@ SCRATCH = {
     "xgp2": ("psum", [128, 1024], "bfloat16"),
     "xgp3": ("psum", [128, 1024], "bfloat16"),
 }
-SEMAPHORES = (["ldw", "ldx", "ldr", "fill", "idn", "ssc", "sxt", "snm", "sex", "srs", "sy0", "sy1", "sev", "st",
-               "sent", "ha", "hs"]
+SEMAPHORES = (["ldd", "ldw", "ldx", "ldr", "fz", "fill", "idn", "ssc", "sxt", "snm", "sex", "srs", "sy0", "sy1",
+               "sev", "st", "sent", "ha", "hs", "pre"]
               + ["a%d" % j for j in range(8)]
               + ["sl%d" % k for k in range(NG)] + ["tr%d" % k for k in range(NG)] + ["xr%d" % k for k in range(NG)])
 
@@ -93,7 +95,7 @@ def rank_program(g, core, T, topo):
                 if not share:
                     continue
                 g.wait_ge(S.ha, NE)
-                _send(g, T, topo, core, T.hw[:], [cores[j] for j in share],
+                _send(g, T, topo, core, T.hd[:], [cores[j] for j in share],
                       T.wall[:, r * 128:(r + 1) * 128], S["a%d" % r], S.hs)
                 g.wait_ge(S.hs, NE)
         return
@@ -118,22 +120,25 @@ def rank_program(g, core, T, topo):
     order = sorted(range(n), key=lambda j: (when(j), j))
     per_g = n // NG
 
-    SY.dma_start(myw, T.w[:, :]).then_inc(S.ldw, 16)
+    SY.dma_start(T.wd[:, :], T.w[:, :]).then_inc(S.ldd, 16)
     SC.dma_start(T.xs[:, 0:Tn], T.x[:, 0:Tn]).then_inc(S.ldx, 16)
     SY.dma_start(T.rts[:, :], T.rt[:, :]).then_inc(S.ldr, 16)
+    SY.dma_start(myw, T.w[:, :]).then_inc(S.ldw, 16)
 
+    V.memset(T.zz[:], 0.0).then_inc(S.fz, 1)
     V.memset(T.ones[:], 1.0).then_inc(S.fill, 1)
-    V.memset(T.ssum[:], 1.0).then_inc(S.fill, 1)
-    g.wait_ge(S.fill, 2)
+    SC.wait_ge(S.fz, 1)
+    SC.activation(T.ssum[:], T.zz[:], ActivationFunctionType.Exp).then_inc(S.pre, 1)
+    g.wait_ge(S.fill, 1)
     g.affine_select(T.ident[:], T.ones[:], [[-1, 128]], AluOpType.is_equal, 0.0, 0, 1).then_inc(S.idn, 1)
 
-    g.wait_ge(S.ldw, 16)
+    g.wait_ge(S.ldd, 16)
     sent = 0
     if me["helpers"]:
-        _send(g, T, topo, core, myw, me["helpers"], T.hw[:], S.ha, S.sent)
+        _send(g, T, topo, core, T.wd[:], me["helpers"], T.hd[:], S.ha, S.sent)
         sent += NE
     if me["direct"]:
-        _send(g, T, topo, core, myw, [cores[j] for j in me["direct"]], myw, S["a%d" % rank], S.sent)
+        _send(g, T, topo, core, T.wd[:], [cores[j] for j in me["direct"]], myw, S["a%d" % rank], S.sent)
         sent += NE
 
     TE.wait_ge(S.ldx, 16)
@@ -149,14 +154,14 @@ def rank_program(g, core, T, topo):
     for b, (s, tb) in enumerate(blocks):
         V.tensor_reduce(T.nm[0:tb, b:b + 1], T.pa[0:tb, 256 + b * 8:256 + (b + 1) * 8], AxisListType.X,
                         AluOpType.max, negate=True).then_inc(S.snm, 1)
-    SC.wait_ge(S.fill, 2)
+    SC.wait_ge(S.pre, 1)
     SC.wait_ge(S.ssc, nb)
     SC.wait_ge(S.snm, nb)
     for b, (s, tb) in enumerate(blocks):
         SC.activation(T.ex[0:tb, b * 8:(b + 1) * 8], T.pa[0:tb, 256 + b * 8:256 + (b + 1) * 8],
                       ActivationFunctionType.Exp, bias=T.nm[0:tb, b:b + 1], scale=1.0,
                       accum_out=T.ssum[0:tb, b:b + 1]).then_inc(S.sex, 1)
-    V.wait_ge(S.fill, 2)
+    V.wait_ge(S.pre, 1)
     V.wait_ge(S.sex, nb)
     V.reciprocal(T.rs[:, 0:nb], T.ssum[:, 0:nb]).then_inc(S.srs, 1)
     V.wait_ge(S.srs, 1)

from concourse.bass import DstId, RemoteDMATransfer
from concourse.mybir import dt, AluOpType, AxisListType, ActivationFunctionType

NH = 2
NE = 8
NG = 4

SCRATCH = {
    "wd": ("dram", [128, 128], "bfloat16"),
    "hd": ("dram", [128, 128], "bfloat16"),
    "wall": ("sbuf", [128, 1024], "bfloat16"),
    "xs": ("sbuf", [128, 256], "bfloat16"),
    "rts": ("sbuf", [128, 8], "bfloat16"),
    "ones": ("sbuf", [128, 128], "bfloat16"),
    "ident": ("sbuf", [128, 128], "bfloat16"),
    "nm": ("sbuf", [128, 2], "float32"),
    "ex": ("sbuf", [128, 16], "float32"),
    "ssum": ("sbuf", [128, 2], "float32"),
    "zz": ("sbuf", [128, 2], "float32"),
    "rs": ("sbuf", [128, 2], "float32"),
    "xtg": ("sbuf", [128, 2048], "bfloat16"),
    "xg": ("sbuf", [128, 2048], "bfloat16"),
    "ysb": ("sbuf", [128, 256], "bfloat16"),
    "pa": ("psum", [128, 512], "float32"),
    "pb": ("psum", [128, 512], "float32"),
    "xtp": ("psum", [128, 1024], "bfloat16"),
    "xgp0": ("psum", [128, 1024], "bfloat16"),
    "xgp1": ("psum", [128, 1024], "bfloat16"),
    "xgp2": ("psum", [128, 1024], "bfloat16"),
    "xgp3": ("psum", [128, 1024], "bfloat16"),
}
SEMAPHORES = (["ldd", "ldw", "ldx", "ldr", "fz", "fill", "idn", "ssc", "sxt", "snm", "sex", "srs", "sy0", "sy1",
               "sev", "st", "sent", "ha", "hs", "pre"]
              + ["a%d" % j for j in range(8)]
              + ["sl%d" % k for k in range(NG)] + ["tr%d" % k for k in range(NG)] + ["xr%d" % k for k in range(NG)])


def _engines(mask, n):
    out, bit = 0, 1
    while n > 0 and bit <= mask:
        if mask & bit:
            out |= bit
            n -= 1
        bit <<= 1
    return out


def _plan(T, topo):
    cores = list(T.cores)
    n = len(cores)
    plan = []
    for r, c in enumerate(cores):
        plane = [j for j in range(n) if j == r or topo.may_write(c, cores[j])]
        cross = [j for j in range(n) if j not in plane]
        k = plane.index(r)
        direct = [plane[(k + i) % len(plane)] for i in range(1, len(plane))]
        if cross:
            s = k % len(cross)
            cross = cross[s:] + cross[:s]
        cand = [h for h in range(topo.CHIPS * topo.CORES_PER_CHIP)
                if topo.chip(h) == topo.chip(c) and h not in cores
                and all(topo.may_write(h, cores[j]) for j in cross)]
        cand.sort(key=lambda h: (topo.die(h) != topo.die(c), h))
        helpers = cand[:NH] if cross else []
        per = (len(cross) + len(helpers) - 1) // len(helpers) if helpers else 0
        shares = [cross[i * per:(i + 1) * per] for i in range(len(helpers))]
        plan.append({"direct": direct, "helpers": helpers, "shares": shares})
    return plan


def _send(g, T, topo, core, src, dst_cores, dst_ap, sem, local_sem):
    mask = 0
    for i, d in enumerate(dst_cores):
        m = topo.mask(core, d)
        mask = m if i == 0 else (mask & m)
    ids = []
    for d in dst_cores:
        rid, pid, _s = topo.addr(d)
        ids.append(DstId(rid=rid, pnc=pid))
    g.remote_dma_fused([RemoteDMATransfer(dst_ids=ids, dma_engine_mask=_engines(mask, NE), remote_sem=sem,
                                          srcs=[src], dsts=[dst_ap for _d in dst_cores], alu_op=0)],
                       local_sem=local_sem)


def rank_program(g, core, T, topo):
    plan = _plan(T, topo)
    cores = list(T.cores)
    S = T.sem
    rank = T.rank_of(core)

    if rank is None:
        for r, p in enumerate(plan):
            if core in p["helpers"]:
                share = p["shares"][p["helpers"].index(core)]
                if not share:
                    continue
                g.wait_ge(S.ha, NE)
                _send(g, T, topo, core, T.hd[:], [cores[j] for j in share],
                      T.wall[:, r * 128:(r + 1) * 128], S["a%d" % r], S.hs)
                g.wait_ge(S.hs, NE)
        return

    me = plan[rank]
    n = len(cores)
    Tn = int(T.tables["WID"][rank])
    blocks = [(s, min(128, Tn - s)) for s in range(0, Tn, 128)]
    nb = len(blocks)
    myw = T.wall[:, rank * 128:(rank + 1) * 128]
    V, SC, TE, SY = g.vector, g.scalar, g.tensor, g.sync

    def when(j):
        if j == rank:
            return (0, 0)
        if rank in plan[j]["direct"]:
            return (1, plan[j]["direct"].index(rank))
        for sh in plan[j]["shares"]:
            if rank in sh:
                return (2, sh.index(rank))
        return (3, 0)
    order = sorted(range(n), key=lambda j: (when(j), j))
    per_g = n // NG

    SY.dma_start(T.wd[:, :], T.w[:, :]).then_inc(S.ldd, 16)
    SC.dma_start(T.xs[:, 0:Tn], T.x[:, 0:Tn]).then_inc(S.ldx, 16)
    SY.dma_start(T.rts[:, :], T.rt[:, :]).then_inc(S.ldr, 16)
    SY.dma_start(myw, T.w[:, :]).then_inc(S.ldw, 16)

    V.memset(T.zz[:], 0.0).then_inc(S.fz, 1)
    V.memset(T.ones[:], 1.0).then_inc(S.fill, 1)
    SC.wait_ge(S.fz, 1)
    SC.activation(T.ssum[:], T.zz[:], ActivationFunctionType.Exp).then_inc(S.pre, 1)
    g.wait_ge(S.fill, 1)
    g.affine_select(T.ident[:], T.ones[:], [[-1, 128]], AluOpType.is_equal, 0.0, 0, 1).then_inc(S.idn, 1)

    g.wait_ge(S.ldd, 16)
    sent = 0
    if me["helpers"]:
        _send(g, T, topo, core, T.wd[:], me["helpers"], T.hd[:], S.ha, S.sent)
        sent += NE
    if me["direct"]:
        _send(g, T, topo, core, T.wd[:], [cores[j] for j in me["direct"]], myw, S["a%d" % rank], S.sent)
        sent += NE

    TE.wait_ge(S.ldx, 16)
    TE.wait_ge(S.ldr, 16)
    for b, (s, tb) in enumerate(blocks):
        TE.matmul(T.pa[0:tb, 256 + b * 8:256 + (b + 1) * 8], T.xs[:, s:s + tb], T.rts[:, :], True, True
                  ).then_inc(S.ssc, 1)
    TE.wait_ge(S.idn, 1)
    for b, (s, tb) in enumerate(blocks):
        TE.transpose(T.xtp[0:tb, b * 128:(b + 1) * 128], T.xs[:, s:s + tb], T.ident[:, :]).then_inc(S.sxt, 1)

    V.wait_ge(S.ssc, nb)
    for b, (s, tb) in enumerate(blocks):
        V.tensor_reduce(T.nm[0:tb, b:b + 1], T.pa[0:tb, 256 + b * 8:256 + (b + 1) * 8], AxisListType.X,
                        AluOpType.max, negate=True).then_inc(S.snm, 1)
    SC.wait_ge(S.pre, 1)
    SC.wait_ge(S.ssc, nb)
    SC.wait_ge(S.snm, nb)
    for b, (s, tb) in enumerate(blocks):
        SC.activation(T.ex[0:tb, b * 8:(b + 1) * 8], T.pa[0:tb, 256 + b * 8:256 + (b + 1) * 8],
                      ActivationFunctionType.Exp, bias=T.nm[0:tb, b:b + 1], scale=1.0,
                      accum_out=T.ssum[0:tb, b:b + 1]).then_inc(S.sex, 1)
    V.wait_ge(S.pre, 1)
    V.wait_ge(S.sex, nb)
    V.reciprocal(T.rs[:, 0:nb], T.ssum[:, 0:nb]).then_inc(S.srs, 1)
    V.wait_ge(S.srs, 1)
    V.wait_ge(S.sxt, nb)

    for k in range(NG):
        for i in range(per_g):
            j = order[k * per_g + i]
            for b, (s, tb) in enumerate(blocks):
                slot = (k * per_g + i) * nb + b
                V.tensor_scalar(T.xtg[0:tb, slot * 128:(slot + 1) * 128], T.xtp[0:tb, b * 128:(b + 1) * 128],
                                T.ex[0:tb, b * 8 + j:b * 8 + j + 1], T.rs[0:tb, b:b + 1],
                                AluOpType.mult, AluOpType.mult).then_inc(S["sl%d" % k], 1)
    for k in range(NG):
        TE.wait_ge(S["sl%d" % k], per_g * nb)
        for i in range(per_g):
            for b, (s, tb) in enumerate(blocks):
                slot = (k * per_g + i) * nb + b
                TE.transpose(T["xgp%d" % k][:, i * Tn + s:i * Tn + s + tb],
                             T.xtg[0:tb, slot * 128:(slot + 1) * 128], T.ident[0:tb, 0:tb]
                             ).then_inc(S["tr%d" % k], 1)
    for k in range(NG):
        out = T.xg[:, k * per_g * Tn:(k + 1) * per_g * Tn]
        src = T["xgp%d" % k][:, 0:per_g * Tn]
        if k % 2 == 0:
            SC.wait_ge(S["tr%d" % k], per_g * nb)
            SC.activation(out, src, ActivationFunctionType.Copy).then_inc(S["xr%d" % k], 1)
        else:
            V.wait_ge(S["tr%d" % k], per_g * nb)
            V.tensor_copy(out, src).then_inc(S["xr%d" % k], 1)

    if Tn >= 128:
        ta = ((Tn // 2 + 7) // 8) * 8
        halves = [(0, ta, T.pa, S.sy0), (ta, Tn, T.pb, S.sy1)]
    else:
        halves = [(0, Tn, T.pa, S.sy0)]
    for i, j in enumerate(order):
        if i % per_g == 0:
            TE.wait_ge(S["xr%d" % (i // per_g)], 1)
        if j == rank:
            TE.wait_ge(S.ldw, 16)
        else:
            TE.wait_ge(S["a%d" % j], NE)
        for (lo, hi, ps, sem) in halves:
            mm = TE.matmul(ps[:, 0:hi - lo], T.wall[:, j * 128:(j + 1) * 128], T.xg[:, i * Tn + lo:i * Tn + hi],
                           i == 0, i == n - 1)
            if i == n - 1:
                mm.then_inc(sem, 1)

    lo, hi, ps, sem = halves[0]
    V.wait_ge(sem, 1)
    V.tensor_copy(T.ysb[:, lo:hi], ps[:, 0:hi - lo]).then_inc(S.sev, 1)
    if len(halves) > 1:
        lo, hi, ps, sem = halves[1]
        SC.wait_ge(sem, 1)
        SC.activation(T.ysb[:, lo:hi], ps[:, 0:hi - lo], ActivationFunctionType.Copy).then_inc(S.sev, 1)
    SY.wait_ge(S.sev, len(halves))
    SY.dma_start(T.y[:, 0:Tn], T.ysb[:, 0:Tn]).then_inc(S.st, 16)
    SY.wait_ge(S.st, 16)
    if sent:
        g.wait_ge(S.sent, sent)
